import numpy as np
import ml_dtypes


def mxq(x, axis, fmt="e4m3"):
    dtype, down = {"e4m3": (ml_dtypes.float8_e4m3fn, 7), "e5m2": (ml_dtypes.float8_e5m2, 14)}[fmt]
    v = np.moveaxis(np.asarray(x, np.float32).astype(ml_dtypes.bfloat16).astype(np.float64), axis, -1)
    blocks = v.reshape(v.shape[:-1] + (-1, 32))
    amax = np.abs(blocks).max(-1, keepdims=True)
    byte = np.maximum(np.where(amax > 0, np.frexp(amax)[1] - 1 + 127, 0) - down, 1)
    scale = np.exp2(byte - 127.0)
    codes = (blocks / scale).astype(np.float32).astype(dtype).astype(np.float64)
    return np.moveaxis((codes * scale).reshape(v.shape), -1, axis)


WIDE = False


def mx_kscale(k):
    if not WIDE:
        return np.ones(k)
    levels = np.array([10, -10, 5, -5, 0])
    if k % 512:
        return np.exp2(np.random.permutation(np.resize(levels, k // 32))).repeat(32)
    a = np.empty((k // 512, 16))
    for p in range(k // 512):
        a[p, :8] = np.random.permutation(np.resize(levels, 8))
        for g in range(8):
            far = levels[np.abs(levels - a[p, g]) >= 10]
            a[p, g + 8] = far[np.random.randint(len(far))]
    return np.exp2(a.ravel()).repeat(32)


def f64(x):
    return np.asarray(x).astype(np.float64)


def striped(idx):
    return np.tile(idx.reshape(-1, 16).T, (8, 1)).astype(np.uint16)


def unstriped(offs):
    return offs[:16].T.reshape(-1).astype(np.int64)


def striped8(idx):
    return np.concatenate([x.reshape(-1, 16).T for x in idx]).astype(np.uint16)


def runs(offs, k):
    lists = np.stack([offs[16 * r : 16 * r + 16].T.reshape(-1) for r in range(8)]).astype(np.int64)
    return lists[np.arange(k) % 512 // 64]


def pack_weight(w):
    k, n = w.shape
    w = f64(np.asarray(w, np.float32).astype(ml_dtypes.bfloat16)).reshape(k // 32, 32, n)
    amax = np.abs(w).max(1)
    byte = np.clip(np.where(amax > 0, np.frexp(amax)[1] - 1 + 127 - 7, 1), 1, 254)
    scaled = (w * np.exp2(127.0 - byte)[:, None, :]).reshape(k, n).astype(np.float32)
    words = np.ascontiguousarray(scaled.reshape(k // 512, 128, 4, n).transpose(0, 1, 3, 2)).astype(ml_dtypes.float8_e4m3fn).view(np.uint8)
    return words, np.ascontiguousarray(byte.astype(np.uint8).reshape(k // 512, 16, n))


def unpack_weight(words, scales):
    g, p, n, _ = words.shape
    vals = np.ascontiguousarray(words).view(ml_dtypes.float8_e4m3fn).astype(np.float64) * np.repeat(np.exp2(scales.astype(np.float64) - 127.0), 8, axis=1)[..., None]
    return vals.transpose(0, 1, 3, 2).reshape(g * 512, n)


K, T, S, N, H, W = 512, 2048, 512, 512, 512, 256


def setup_inputs():
    n = np.random.standard_normal
    s = mx_kscale(K)[:, None]
    u = mx_kscale(H)
    packed_xT = pack_weight(n((K, T)) * s)
    perm = np.stack([np.random.permutation(S) for _ in range(8)])
    return {
        "x_words": packed_xT[0],
        "x_scales": packed_xT[1],
        "w1": (n((K, H)) / np.sqrt(K) / s).astype(np.float32),
        "gn": (np.random.uniform(0.5, 1.5, (H, 1)) * u[:, None]).astype(np.float32),
        "w2": (n((H, N)) / np.sqrt(H) / u[:, None]).astype(np.float32),
        "offs": striped(np.random.permutation(T)[:S]),
        "n1": striped8(perm[:, :W]),
        "n2": striped8(perm[:, W:]),
        "n3": striped8(np.stack([np.random.permutation(S) for _ in range(8)])),
        "n4": striped8(np.stack([np.random.permutation(S) for _ in range(8)])),
    }


def reference(x_words, x_scales, w1, gn, w2, offs, n1, n2, n3, n4):
    xq = unpack_weight(x_words, x_scales)[:, unstriped(offs)]
    y = mxq(f64(w1), 0, "e4m3").T @ xq
    pb = y[np.arange(H)[:, None], runs(n2, H)]
    pa = y[np.arange(H)[:, None], runs(n1, H)]
    rb = pb - (0.5 * pa)
    ra = np.sqrt((pa) ** 2 + (pb) ** 2 + 0.25)
    ds = np.zeros((H, S))
    ds[np.arange(H)[:, None], runs(n1, H)] = ra
    dt = ds.copy()
    dt[np.arange(H)[:, None], runs(n2, H)] = rb
    z = f64(gn) * dt
    h = mxq(f64(w2), 0, "e4m3").T @ mxq(z, 0, "e4m3")
    st = h + 0.5 * (h[np.arange(N)[:, None], runs(n3, N)])
    return st - (st[np.arange(N)[:, None], runs(n4, N)])

@@ -1,0 +1,198 @@
+from contextlib import ExitStack
+
+import concourse.mybir as mybir
+
+K, T, S, N, H, W = 512, 2048, 512, 512, 512, 256
+FLOPS = 2 * K * H * S + 2 * H * N * S
+
+F32 = mybir.dt.float32
+BF16 = mybir.dt.bfloat16
+I32 = mybir.dt.int32
+U32 = mybir.dt.uint32
+U16 = mybir.dt.uint16
+U8 = mybir.dt.uint8
+FP8X4 = mybir.dt.float8_e4m3fn_x4
+ACT = mybir.ActivationFunctionType
+ALU = mybir.AluOpType
+
+P = 128
+PACK = 4
+HALF = S // 2
+COLS16 = HALF // 16
+SLOT_ORDER = (0, 2, 3, 1)
+
+
+def tile_picked_laypolarhop_none_p_kernel(
+    tc, x_words, x_scales, w1, gn, w2, offs, n1, n2, n3, n4, out
+):
+    nc = tc.nc
+    with ExitStack() as ctx:
+        lists = ctx.enter_context(tc.tile_pool(name="lists", bufs=1))
+        keep = ctx.enter_context(tc.tile_pool(name="keep", bufs=1))
+        ring = ctx.enter_context(tc.tile_pool(name="ring", bufs=2))
+        psum = ctx.enter_context(tc.psum_pool(name="psum", bufs=8))
+
+        def halves():
+            return [(a, slice(a * HALF, (a + 1) * HALF), slice(a * COLS16, (a + 1) * COLS16)) for a in range(2)]
+
+        offs_sb = lists.tile([P, S // 16], U16, name="offs_sb")
+        n1_sb = lists.tile([P, W // 16], U16, name="n1_sb")
+        n2_sb = lists.tile([P, W // 16], U16, name="n2_sb")
+        n3_sb = lists.tile([P, S // 16], U16, name="n3_sb")
+        n4_sb = lists.tile([P, S // 16], U16, name="n4_sb")
+        w1_raw = keep.tile([P, PACK, H], F32, name="w1_raw")
+        w2_raw = keep.tile([P, PACK, N], F32, name="w2_raw")
+        x_tab = keep.tile([P, T], U32, name="x_tab")
+        xs_tab = keep.tile([P, T], U8, name="xs_tab")
+        gain = keep.tile([P, PACK], F32, name="gain")
+
+        nc.vector.memset(xs_tab[:].bitcast(I32), 0)
+        nc.sync.dma_start(offs_sb[:], offs)
+        nc.sync.dma_start(w1_raw[:], w1.rearrange("(p j) c -> p j c", j=PACK))
+        for q in range(4):
+            nc.sync.dma_start(
+                xs_tab[32 * q : 32 * q + 4, :].bitcast(I32), x_scales[0, 4 * q : 4 * q + 4, :].bitcast(I32)
+            )
+        nc.sync.dma_start(x_tab[:].bitcast(I32), x_words[0].rearrange("p n t -> p (n t)").bitcast(I32))
+        warm = keep.tile([P, 2], F32, name="warm")
+        nc.vector.memset(warm[:, 0:1], 1.0)
+        nc.scalar.activation(warm[:, 1:2], warm[:, 0:1], ACT.Sqrt)
+        nc.sync.dma_start(n1_sb[:], n1)
+        nc.sync.dma_start(n2_sb[:], n2)
+        nc.sync.dma_start(w2_raw[:], w2.rearrange("(p j) c -> p j c", j=PACK))
+        nc.sync.dma_start(gain[:], gn.rearrange("(p t) o -> p (t o)", t=PACK))
+        nc.sync.dma_start(n3_sb[:], n3)
+        nc.sync.dma_start(n4_sb[:], n4)
+
+        def deal(engine_copy, grouped, raw, m0, m1):
+            engine_copy(
+                grouped[:].rearrange("p (t m j) -> p m t j", t=PACK, j=PACK)[:, m0:m1],
+                raw[:].rearrange("p j (m t) -> p m t j", t=PACK)[:, m0:m1],
+            )
+
+        xg_scales = keep.tile([P, S], U8, name="xg_scales", align_bytes=64)
+        nc.vector.tensor_copy(xg_scales[:], xs_tab[:].indirect(offs_sb[:]))
+
+        w1_bf = keep.tile([P, PACK * H], BF16, name="w1_bf", align_bytes=64)
+        deal(nc.vector.tensor_copy, w1_bf, w1_raw, 0, 96)
+        deal(nc.scalar.copy, w1_bf, w1_raw, 96, 128)
+        w1_codes = keep.tile([P, H], U32, name="w1_codes", align_bytes=64)
+        w1_scales = keep.tile([P, H], U8, name="w1_scales", align_bytes=64)
+        nc.vector.quantize_mx(w1_codes[:].bitcast(FP8X4), w1_scales[:], w1_bf[:])
+
+        xg_words = keep.tile([P, S], U32, name="xg_words", align_bytes=64)
+        for a, cols, lcols in halves():
+            nc.vector.tensor_copy(xg_words[:, cols], x_tab[:].indirect(offs_sb[:, lcols]))
+
+        def product(codes, scales, t, rhs, rhs_scales, cols, width):
+            acc = psum.tile([P, width], F32, name="acc")
+            m = slice(t * P, (t + 1) * P)
+            nc.tensor.matmul_mx(
+                acc[:], lhsT=codes[:, m].bitcast(FP8X4), lhsT_scale=scales[:, m],
+                rhs=rhs[:, cols].bitcast(FP8X4), rhs_scale=rhs_scales[:, cols], start=True, stop=True,
+            )
+            return acc
+
+        y = {t: keep.tile([P, S], F32, name=f"y{t}") for t in SLOT_ORDER}
+        d = {t: keep.tile([P, S], F32, name=f"d{t}") for t in SLOT_ORDER}
+        first = SLOT_ORDER[0]
+        for a, cols, lcols in halves():
+            acc = product(w1_codes, w1_scales, first, xg_words, xg_scales, cols, HALF)
+            nc.scalar.copy(y[first][:, cols], acc[:])
+
+        def make_y(t):
+            acc = product(w1_codes, w1_scales, t, xg_words, xg_scales, slice(0, S), S)
+            nc.scalar.copy(y[t][:], acc[:])
+
+        z_bf = keep.tile([P, S, PACK], BF16, name="z_bf", align_bytes=64)
+        w2_bf = keep.tile([P, PACK * N], BF16, name="w2_bf", align_bytes=64)
+        roots = {}
+
+        def put_roots(t):
+            nc.vector.tensor_copy(d[t][:].indirect(n1_sb[:]), roots[t][:])
+
+        def write_z(t, cols):
+            nc.scalar.activation(z_bf[:, cols, t], d[t][:, cols], ACT.Copy, scale=gain[:, t : t + 1])
+
+        for i, t in enumerate(SLOT_ORDER):
+            last = i == PACK - 1
+            if not last:
+                make_y(SLOT_ORDER[i + 1])
+            pair = keep.tile([P, 2 * W], F32, name="pair")
+            nc.vector.tensor_copy(pair[:, :W], y[t][:].indirect(n1_sb[:]))
+            nc.vector.tensor_copy(pair[:, W:], y[t][:].indirect(n2_sb[:]))
+            minus_half = ring.tile([P, W], F32, name="minus_half")
+            nc.scalar.activation(minus_half[:], pair[:, :W], ACT.Copy, scale=-0.5)
+            squares = ring.tile([P, 2 * W], F32, name="squares")
+            nc.scalar.activation(squares[:], pair[:], ACT.Square)
+            if i > 0:
+                put_roots(SLOT_ORDER[i - 1])
+            radicand = ring.tile([P, W], F32, name="radicand")
+
+            def put_differences():
+                nc.vector.tensor_tensor(d[t][:].indirect(n2_sb[:]), pair[:, W:], minus_half[:], ALU.add)
+
+            def add_squares():
+                nc.vector.scalar_tensor_tensor(radicand[:], squares[:, :W], 0.25, squares[:, W:], ALU.add, ALU.add)
+
+            for step in (add_squares, put_differences) if last else (put_differences, add_squares):
+                step()
+            if i > 0:
+                write_z(SLOT_ORDER[i - 1], slice(0, S))
+            roots[t] = ring.tile([P, W], F32, name="root")
+            nc.scalar.activation(roots[t][:], radicand[:], ACT.Sqrt)
+            deal(nc.scalar.copy, w2_bf, w2_raw, 32 * i, 32 * (i + 1))
+
+        w2_codes = keep.tile([P, N], U32, name="w2_codes", align_bytes=64)
+        w2_scales = keep.tile([P, N], U8, name="w2_scales", align_bytes=64)
+        nc.vector.quantize_mx(w2_codes[:].bitcast(FP8X4), w2_scales[:], w2_bf[:])
+
+        t = SLOT_ORDER[-1]
+        put_roots(t)
+        nc.vector.tensor_scalar(z_bf[:, :HALF, t], d[t][:, :HALF], gain[:, t : t + 1], None, ALU.mult)
+        write_z(t, slice(HALF, S))
+
+        z_codes = keep.tile([P, S], U32, name="z_codes", align_bytes=64)
+        z_scales = keep.tile([P, S], U8, name="z_scales", align_bytes=64)
+        for a, cols, lcols in halves():
+            nc.vector.quantize_mx(
+                z_codes[:, cols].bitcast(FP8X4), z_scales[:, cols], z_bf[:, cols, :].rearrange("p s j -> p (s j)")
+            )
+
+        h = [keep.tile([P, S], F32, name=f"h{t}") for t in range(PACK)]
+        h_half = [keep.tile([P, S], F32, name=f"h_half{t}") for t in range(PACK)]
+        st = [keep.tile([P, S], F32, name=f"st{t}") for t in range(PACK)]
+        minus_st = [keep.tile([P, S], F32, name=f"minus_st{t}") for t in range(PACK)]
+        res = [keep.tile([P, S], F32, name=f"res{t}") for t in range(PACK)]
+        out_rows = out.rearrange("(p t) n -> p t n", t=PACK)
+
+        def make_h(t):
+            if t == 0:
+                parts = [(cols, product(w2_codes, w2_scales, t, z_codes, z_scales, cols, HALF)) for a, cols, lcols in halves()]
+            else:
+                parts = [(slice(0, S), product(w2_codes, w2_scales, t, z_codes, z_scales, slice(0, S), S))]
+            for cols, acc in parts:
+                nc.scalar.activation(h_half[t][:, cols], acc[:], ACT.Copy, scale=0.5)
+                nc.scalar.copy(h[t][:, cols], acc[:])
+
+        def first_hop(t):
+            for a, cols, lcols in halves():
+                nc.vector.tensor_tensor(st[t][:, cols], h_half[t][:].indirect(n3_sb[:, lcols]), h[t][:, cols], ALU.add)
+
+        def negate(t):
+            nc.scalar.activation(minus_st[t][:], st[t][:], ACT.Copy, scale=-1.0)
+
+        def second_hop(t):
+            for a, cols, lcols in halves():
+                nc.vector.tensor_tensor(res[t][:, cols], minus_st[t][:].indirect(n4_sb[:, lcols]), st[t][:, cols], ALU.add)
+                nc.sync.dma_start(out_rows[:, t, cols], res[t][:, cols])
+
+        make_h(0)
+        first_hop(0)
+        for t in range(1, PACK):
+            make_h(t)
+            negate(t - 1)
+            first_hop(t)
+            second_hop(t - 1)
+        negate(PACK - 1)
+        second_hop(PACK - 1)

@@ -42,7 +42,7 @@ def tile_picked_laypolarhop_none_p_kernel(
         n4_sb = lists.tile([P, S // 16], U16, name="n4_sb")
         w1_raw = keep.tile([P, PACK, H], F32, name="w1_raw")
         w2_raw = keep.tile([P, PACK, N], F32, name="w2_raw")
-        x_tab = keep.tile([P, T], U32, name="x_tab")
+        x_tab = keep.tile([P, T], U32, name="x_tab", tag="x_tab", align_bytes=64)
         xs_tab = keep.tile([P, T], U8, name="xs_tab")
         gain = keep.tile([P, PACK], F32, name="gain")
 
@@ -54,9 +54,10 @@ def tile_picked_laypolarhop_none_p_kernel(
                 xs_tab[32 * q : 32 * q + 4, :].bitcast(I32), x_scales[0, 4 * q : 4 * q + 4, :].bitcast(I32)
             )
         nc.sync.dma_start(x_tab[:].bitcast(I32), x_words[0].rearrange("p n t -> p (n t)").bitcast(I32))
-        warm = keep.tile([P, 2], F32, name="warm")
-        nc.vector.memset(warm[:, 0:1], 1.0)
-        nc.scalar.activation(warm[:, 1:2], warm[:, 0:1], ACT.Sqrt)
+        quarter = keep.tile([P, 1], F32, name="quarter")
+        nc.vector.memset(quarter[:], 0.25)
+        warm = keep.tile([P, 1], F32, name="warm")
+        nc.scalar.activation(warm[:], quarter[:], ACT.Sqrt)
         nc.sync.dma_start(n1_sb[:], n1)
         nc.sync.dma_start(n2_sb[:], n2)
         nc.sync.dma_start(w2_raw[:], w2.rearrange("(p j) c -> p j c", j=PACK))
@@ -71,38 +72,49 @@ def tile_picked_laypolarhop_none_p_kernel(
             )
 
         xg_scales = keep.tile([P, S], U8, name="xg_scales", align_bytes=64)
-        nc.vector.tensor_copy(xg_scales[:], xs_tab[:].indirect(offs_sb[:]))
 
         w1_bf = keep.tile([P, PACK * H], BF16, name="w1_bf", align_bytes=64)
-        deal(nc.vector.tensor_copy, w1_bf, w1_raw, 0, 96)
-        deal(nc.scalar.copy, w1_bf, w1_raw, 96, 128)
-        w1_codes = keep.tile([P, H], U32, name="w1_codes", align_bytes=64)
+        w1_to = w1_bf[:].rearrange("p (t m j) -> p m t j", t=PACK, j=PACK)
+        w1_from = w1_raw[:].rearrange("p j (m t) -> p m t j", t=PACK)
+        nc.vector.tensor_copy(w1_to[:, :, 0], w1_from[:, :, 0])
+        nc.scalar.copy(w1_to[:, :, 1:], w1_from[:, :, 1:])
+        nc.vector.tensor_copy(xg_scales[:], xs_tab[:].indirect(offs_sb[:]))
+        w1_codes = keep.tile([P, P], U32, name="w1_codes", align_bytes=64)
         w1_scales = keep.tile([P, H], U8, name="w1_scales", align_bytes=64)
-        nc.vector.quantize_mx(w1_codes[:].bitcast(FP8X4), w1_scales[:], w1_bf[:])
+        nc.vector.quantize_mx(w1_codes[:].bitcast(FP8X4), w1_scales[:, :P], w1_bf[:, : PACK * P])
 
         xg_words = keep.tile([P, S], U32, name="xg_words", align_bytes=64)
         for a, cols, lcols in halves():
             nc.vector.tensor_copy(xg_words[:, cols], x_tab[:].indirect(offs_sb[:, lcols]))
 
+        w1_rest = keep.tile([P, H - P], U32, name="w1_rest", tag="x_tab", align_bytes=64)
+        for c0, c1 in ((P, 2 * P), (2 * P, H)):
+            nc.vector.quantize_mx(
+                w1_rest[:, c0 - P : c1 - P].bitcast(FP8X4), w1_scales[:, c0:c1], w1_bf[:, PACK * c0 : PACK * c1]
+            )
+        w1_tiles = [w1_codes[:]] + [w1_rest[:, t * P : (t + 1) * P] for t in range(PACK - 1)]
+
         def product(codes, scales, t, rhs, rhs_scales, cols, width):
             acc = psum.tile([P, width], F32, name="acc")
             m = slice(t * P, (t + 1) * P)
             nc.tensor.matmul_mx(
-                acc[:], lhsT=codes[:, m].bitcast(FP8X4), lhsT_scale=scales[:, m],
+                acc[:], lhsT=codes[t].bitcast(FP8X4), lhsT_scale=scales[:, m],
                 rhs=rhs[:, cols].bitcast(FP8X4), rhs_scale=rhs_scales[:, cols], start=True, stop=True,
             )
             return acc
 
-        y = {t: keep.tile([P, S], F32, name=f"y{t}") for t in SLOT_ORDER}
+        y = keep.tile([P, S], F32, name="y")
+        pair = keep.tile([P, 2 * W], F32, name="pair")
+        scratch = [keep.tile([P, W], F32, name=f"scratch{b}") for b in range(2)]
         d = {t: keep.tile([P, S], F32, name=f"d{t}") for t in SLOT_ORDER}
         first = SLOT_ORDER[0]
         for a, cols, lcols in halves():
-            acc = product(w1_codes, w1_scales, first, xg_words, xg_scales, cols, HALF)
-            nc.scalar.copy(y[first][:, cols], acc[:])
+            acc = product(w1_tiles, w1_scales, first, xg_words, xg_scales, cols, HALF)
+            nc.scalar.copy(y[:, cols], acc[:])
 
         def make_y(t):
-            acc = product(w1_codes, w1_scales, t, xg_words, xg_scales, slice(0, S), S)
-            nc.scalar.copy(y[t][:], acc[:])
+            acc = product(w1_tiles, w1_scales, t, xg_words, xg_scales, slice(0, S), S)
+            nc.scalar.copy(y[:], acc[:])
 
         z_bf = keep.tile([P, S, PACK], BF16, name="z_bf", align_bytes=64)
         w2_bf = keep.tile([P, PACK * N], BF16, name="w2_bf", align_bytes=64)
@@ -114,85 +126,100 @@ def tile_picked_laypolarhop_none_p_kernel(
         def write_z(t, cols):
             nc.scalar.activation(z_bf[:, cols, t], d[t][:, cols], ACT.Copy, scale=gain[:, t : t + 1])
 
+        w2_codes = keep.tile([P, N], U32, name="w2_codes", align_bytes=64)
+        w2_scales = keep.tile([P, N], U8, name="w2_scales", align_bytes=64)
+        w2_tiles = [w2_codes[:, t * P : (t + 1) * P] for t in range(PACK)]
+
         for i, t in enumerate(SLOT_ORDER):
             last = i == PACK - 1
-            if not last:
-                make_y(SLOT_ORDER[i + 1])
-            pair = keep.tile([P, 2 * W], F32, name="pair")
-            nc.vector.tensor_copy(pair[:, :W], y[t][:].indirect(n1_sb[:]))
-            nc.vector.tensor_copy(pair[:, W:], y[t][:].indirect(n2_sb[:]))
-            minus_half = ring.tile([P, W], F32, name="minus_half")
+            minus_half, radicand = scratch[(i + 1) % 2], scratch[i % 2]
+            nc.vector.tensor_copy(pair[:, :W], y[:].indirect(n1_sb[:]))
+            nc.vector.tensor_copy(pair[:, W:], y[:].indirect(n2_sb[:]))
             nc.scalar.activation(minus_half[:], pair[:, :W], ACT.Copy, scale=-0.5)
             squares = ring.tile([P, 2 * W], F32, name="squares")
             nc.scalar.activation(squares[:], pair[:], ACT.Square)
+            nc.gpsimd.tensor_tensor(radicand[:], squares[:, :W], squares[:, W:], ALU.add)
             if i > 0:
                 put_roots(SLOT_ORDER[i - 1])
-            radicand = ring.tile([P, W], F32, name="radicand")
-
-            def put_differences():
-                nc.vector.tensor_tensor(d[t][:].indirect(n2_sb[:]), pair[:, W:], minus_half[:], ALU.add)
-
-            def add_squares():
-                nc.vector.scalar_tensor_tensor(radicand[:], squares[:, :W], 0.25, squares[:, W:], ALU.add, ALU.add)
-
-            for step in (add_squares, put_differences) if last else (put_differences, add_squares):
-                step()
+            nc.vector.tensor_tensor(d[t][:].indirect(n2_sb[:]), pair[:, W:], minus_half[:], ALU.add)
+            if last:
+                deal(nc.scalar.copy, w2_bf, w2_raw, 32 * i, 32 * (i + 1))
+            else:
+                make_y(SLOT_ORDER[i + 1])
             if i > 0:
                 write_z(SLOT_ORDER[i - 1], slice(0, S))
             roots[t] = ring.tile([P, W], F32, name="root")
-            nc.scalar.activation(roots[t][:], radicand[:], ACT.Sqrt)
-            deal(nc.scalar.copy, w2_bf, w2_raw, 32 * i, 32 * (i + 1))
+            nc.scalar.activation(roots[t][:], radicand[:], ACT.Sqrt, bias=quarter[:])
+            if not last:
+                deal(nc.scalar.copy, w2_bf, w2_raw, 32 * i, 32 * (i + 1))
 
-        w2_codes = keep.tile([P, N], U32, name="w2_codes", align_bytes=64)
-        w2_scales = keep.tile([P, N], U8, name="w2_scales", align_bytes=64)
         nc.vector.quantize_mx(w2_codes[:].bitcast(FP8X4), w2_scales[:], w2_bf[:])
 
         t = SLOT_ORDER[-1]
         put_roots(t)
-        nc.vector.tensor_scalar(z_bf[:, :HALF, t], d[t][:, :HALF], gain[:, t : t + 1], None, ALU.mult)
-        write_z(t, slice(HALF, S))
+        early, wide, late = slice(HALF, HALF + P), slice(0, HALF), slice(HALF + P, S)
+        nc.vector.tensor_scalar(z_bf[:, wide, t], d[t][:, wide], gain[:, t : t + 1], None, ALU.mult)
+        write_z(t, early)
+        write_z(t, late)
 
         z_codes = keep.tile([P, S], U32, name="z_codes", align_bytes=64)
         z_scales = keep.tile([P, S], U8, name="z_scales", align_bytes=64)
-        for a, cols, lcols in halves():
+        for cols in (early, wide, late):
             nc.vector.quantize_mx(
                 z_codes[:, cols].bitcast(FP8X4), z_scales[:, cols], z_bf[:, cols, :].rearrange("p s j -> p (s j)")
             )
 
-        h = [keep.tile([P, S], F32, name=f"h{t}") for t in range(PACK)]
-        h_half = [keep.tile([P, S], F32, name=f"h_half{t}") for t in range(PACK)]
-        st = [keep.tile([P, S], F32, name=f"st{t}") for t in range(PACK)]
-        minus_st = [keep.tile([P, S], F32, name=f"minus_st{t}") for t in range(PACK)]
+        whole = slice(0, S)
+        half_win = [keep.tile([P, S if t == 0 else 2 * S], F32, name=f"half_win{t}") for t in range(PACK)]
+        minus_win = [keep.tile([P, 2 * S if t in (1, 2) else S], F32, name=f"minus_win{t}") for t in range(PACK)]
+        h_last = keep.tile([P, S], F32, name="h_last")
+        st_late = [keep.tile([P, S], F32, name=f"st_late{t}") for t in range(2)]
+        h = [half_win[1][:, S:], half_win[2][:, S:], half_win[3][:, S:], h_last[:]]
+        st = [minus_win[1][:, S:], minus_win[2][:, S:], st_late[0][:], st_late[1][:]]
         res = [keep.tile([P, S], F32, name=f"res{t}") for t in range(PACK)]
         out_rows = out.rearrange("(p t) n -> p t n", t=PACK)
 
-        def make_h(t):
-            if t == 0:
-                parts = [(cols, product(w2_codes, w2_scales, t, z_codes, z_scales, cols, HALF)) for a, cols, lcols in halves()]
-            else:
-                parts = [(slice(0, S), product(w2_codes, w2_scales, t, z_codes, z_scales, slice(0, S), S))]
-            for cols, acc in parts:
-                nc.scalar.activation(h_half[t][:, cols], acc[:], ACT.Copy, scale=0.5)
-                nc.scalar.copy(h[t][:, cols], acc[:])
+        def entries(cols):
+            return slice(cols.start // 16, cols.stop // 16)
 
-        def first_hop(t):
-            for a, cols, lcols in halves():
-                nc.vector.tensor_tensor(st[t][:, cols], h_half[t][:].indirect(n3_sb[:, lcols]), h[t][:, cols], ALU.add)
+        def h_product(t, cols):
+            return product(w2_tiles, w2_scales, t, z_codes, z_scales, cols, cols.stop - cols.start)
+
+        def halve(t, cols, acc):
+            nc.scalar.activation(half_win[t][:, cols], acc[:], ACT.Copy, scale=0.5)
+
+        def keep_h(t, cols, acc):
+            nc.scalar.copy(h[t][:, cols], acc[:])
+
+        def first_hop(t, cols):
+            nc.vector.tensor_tensor(st[t][:, cols], half_win[t][:].indirect(n3_sb[:, entries(cols)]), h[t][:, cols], ALU.add)
 
         def negate(t):
-            nc.scalar.activation(minus_st[t][:], st[t][:], ACT.Copy, scale=-1.0)
+            nc.scalar.activation(minus_win[t][:, :S], st[t], ACT.Copy, scale=-1.0)
 
         def second_hop(t):
-            for a, cols, lcols in halves():
-                nc.vector.tensor_tensor(res[t][:, cols], minus_st[t][:].indirect(n4_sb[:, lcols]), st[t][:, cols], ALU.add)
+            pieces = [whole] if t in (1, 2) else [slice(0, HALF), slice(HALF, S)]
+            for cols in pieces:
+                nc.vector.tensor_tensor(
+                    res[t][:, cols], minus_win[t][:].indirect(n4_sb[:, entries(cols)]), st[t][:, cols], ALU.add
+                )
                 nc.sync.dma_start(out_rows[:, t, cols], res[t][:, cols])
 
-        make_h(0)
-        first_hop(0)
+        acc_early, acc_wide, acc_late = h_product(0, early), h_product(0, wide), h_product(0, late)
+        halve(0, early, acc_early)
+        keep_h(0, early, acc_early)
+        halve(0, wide, acc_wide)
+        halve(0, late, acc_late)
+        keep_h(0, wide, acc_wide)
+        keep_h(0, late, acc_late)
+        for cols in (early, wide, late):
+            first_hop(0, cols)
         for t in range(1, PACK):
-            make_h(t)
+            acc = h_product(t, whole)
+            halve(t, whole, acc)
+            keep_h(t, whole, acc)
             negate(t - 1)
-            first_hop(t)
+            first_hop(t, whole)
             second_hop(t - 1)
         negate(PACK - 1)
         second_hop(PACK - 1)

@@ -47,17 +47,17 @@ def tile_picked_laypolarhop_none_p_kernel(
         gain = keep.tile([P, PACK], F32, name="gain")
 
         nc.vector.memset(xs_tab[:].bitcast(I32), 0)
-        nc.sync.dma_start(offs_sb[:], offs)
         nc.sync.dma_start(w1_raw[:], w1.rearrange("(p j) c -> p j c", j=PACK))
+        nc.sync.dma_start(offs_sb[:], offs)
         for q in range(4):
             nc.sync.dma_start(
                 xs_tab[32 * q : 32 * q + 4, :].bitcast(I32), x_scales[0, 4 * q : 4 * q + 4, :].bitcast(I32)
             )
         nc.sync.dma_start(x_tab[:].bitcast(I32), x_words[0].rearrange("p n t -> p (n t)").bitcast(I32))
+        sixteenth = keep.tile([P, 1], F32, name="sixteenth")
+        nc.vector.memset(sixteenth[:], 0.0625)
         quarter = keep.tile([P, 1], F32, name="quarter")
-        nc.vector.memset(quarter[:], 0.25)
-        warm = keep.tile([P, 1], F32, name="warm")
-        nc.scalar.activation(warm[:], quarter[:], ACT.Sqrt)
+        nc.scalar.activation(quarter[:], sixteenth[:], ACT.Sqrt)
         nc.sync.dma_start(n1_sb[:], n1)
         nc.sync.dma_start(n2_sb[:], n2)
         nc.sync.dma_start(w2_raw[:], w2.rearrange("(p j) c -> p j c", j=PACK))
@@ -106,10 +106,10 @@ def tile_picked_laypolarhop_none_p_kernel(
         y = keep.tile([P, S], F32, name="y")
         pair = keep.tile([P, 2 * W], F32, name="pair")
         scratch = [keep.tile([P, W], F32, name=f"scratch{b}") for b in range(2)]
-        d = {t: keep.tile([P, S], F32, name=f"d{t}") for t in SLOT_ORDER}
+        d = {t: keep.tile([P, S], F32, name=f"d{t}", tag=f"d{t}", align_bytes=64) for t in SLOT_ORDER}
         first = SLOT_ORDER[0]
-        for a, cols, lcols in halves():
-            acc = product(w1_tiles, w1_scales, first, xg_words, xg_scales, cols, HALF)
+        for cols in (slice(0, HALF), slice(HALF, HALF + P), slice(HALF + P, S)):
+            acc = product(w1_tiles, w1_scales, first, xg_words, xg_scales, cols, cols.stop - cols.start)
             nc.scalar.copy(y[:, cols], acc[:])
 
         def make_y(t):
@@ -126,18 +126,17 @@ def tile_picked_laypolarhop_none_p_kernel(
         def write_z(t, cols):
             nc.scalar.activation(z_bf[:, cols, t], d[t][:, cols], ACT.Copy, scale=gain[:, t : t + 1])
 
-        w2_codes = keep.tile([P, N], U32, name="w2_codes", align_bytes=64)
+        w2_codes = keep.tile([P, 2 * P], U32, name="w2_codes", align_bytes=64)
         w2_scales = keep.tile([P, N], U8, name="w2_scales", align_bytes=64)
-        w2_tiles = [w2_codes[:, t * P : (t + 1) * P] for t in range(PACK)]
 
         for i, t in enumerate(SLOT_ORDER):
             last = i == PACK - 1
             minus_half, radicand = scratch[(i + 1) % 2], scratch[i % 2]
             nc.vector.tensor_copy(pair[:, :W], y[:].indirect(n1_sb[:]))
             nc.vector.tensor_copy(pair[:, W:], y[:].indirect(n2_sb[:]))
-            nc.scalar.activation(minus_half[:], pair[:, :W], ACT.Copy, scale=-0.5)
             squares = ring.tile([P, 2 * W], F32, name="squares")
             nc.scalar.activation(squares[:], pair[:], ACT.Square)
+            nc.scalar.activation(minus_half[:], pair[:, :W], ACT.Copy, scale=-0.5)
             nc.gpsimd.tensor_tensor(radicand[:], squares[:, :W], squares[:, W:], ALU.add)
             if i > 0:
                 put_roots(SLOT_ORDER[i - 1])
@@ -146,28 +145,34 @@ def tile_picked_laypolarhop_none_p_kernel(
                 deal(nc.scalar.copy, w2_bf, w2_raw, 32 * i, 32 * (i + 1))
             else:
                 make_y(SLOT_ORDER[i + 1])
-            if i > 0:
-                write_z(SLOT_ORDER[i - 1], slice(0, S))
             roots[t] = ring.tile([P, W], F32, name="root")
             nc.scalar.activation(roots[t][:], radicand[:], ACT.Sqrt, bias=quarter[:])
+            if i > 0:
+                write_z(SLOT_ORDER[i - 1], slice(0, S))
             if not last:
                 deal(nc.scalar.copy, w2_bf, w2_raw, 32 * i, 32 * (i + 1))
 
-        nc.vector.quantize_mx(w2_codes[:].bitcast(FP8X4), w2_scales[:], w2_bf[:])
+        nc.vector.quantize_mx(w2_codes[:].bitcast(FP8X4), w2_scales[:, : 2 * P], w2_bf[:, : PACK * 2 * P])
 
         t = SLOT_ORDER[-1]
         put_roots(t)
         early, wide, late = slice(HALF, HALF + P), slice(0, HALF), slice(HALF + P, S)
-        nc.vector.tensor_scalar(z_bf[:, wide, t], d[t][:, wide], gain[:, t : t + 1], None, ALU.mult)
-        write_z(t, early)
-        write_z(t, late)
+        quarters = [slice(c * P, (c + 1) * P) for c in (0, 2, 1, 3)]
+        for cols in quarters[0::2]:
+            nc.vector.tensor_scalar(z_bf[:, cols, t], d[t][:, cols], gain[:, t : t + 1], None, ALU.mult)
+        for cols in quarters[1::2]:
+            write_z(t, cols)
 
         z_codes = keep.tile([P, S], U32, name="z_codes", align_bytes=64)
         z_scales = keep.tile([P, S], U8, name="z_scales", align_bytes=64)
-        for cols in (early, wide, late):
+        for cols in quarters:
             nc.vector.quantize_mx(
                 z_codes[:, cols].bitcast(FP8X4), z_scales[:, cols], z_bf[:, cols, :].rearrange("p s j -> p (s j)")
             )
+
+        w2_rest = keep.tile([P, 2 * P], U32, name="w2_rest", tag=f"d{t}", align_bytes=64)
+        nc.vector.quantize_mx(w2_rest[:].bitcast(FP8X4), w2_scales[:, 2 * P :], w2_bf[:, PACK * 2 * P :])
+        w2_tiles = [w2_codes[:, :P], w2_codes[:, P:], w2_rest[:, :P], w2_rest[:, P:]]
 
         whole = slice(0, S)
         half_win = [keep.tile([P, S if t == 0 else 2 * S], F32, name=f"half_win{t}") for t in range(PACK)]
@@ -198,28 +203,30 @@ def tile_picked_laypolarhop_none_p_kernel(
             nc.scalar.activation(minus_win[t][:, :S], st[t], ACT.Copy, scale=-1.0)
 
         def second_hop(t):
-            pieces = [whole] if t in (1, 2) else [slice(0, HALF), slice(HALF, S)]
+            pieces = [whole] if t in (1, 2) else [wide, slice(HALF, S)] if t == 0 else [wide, early, late]
             for cols in pieces:
                 nc.vector.tensor_tensor(
                     res[t][:, cols], minus_win[t][:].indirect(n4_sb[:, entries(cols)]), st[t][:, cols], ALU.add
                 )
                 nc.sync.dma_start(out_rows[:, t, cols], res[t][:, cols])
 
-        acc_early, acc_wide, acc_late = h_product(0, early), h_product(0, wide), h_product(0, late)
-        halve(0, early, acc_early)
-        keep_h(0, early, acc_early)
-        halve(0, wide, acc_wide)
-        halve(0, late, acc_late)
-        keep_h(0, wide, acc_wide)
-        keep_h(0, late, acc_late)
-        for cols in (early, wide, late):
+        accs = [h_product(0, cols) for cols in quarters]
+        for cols, acc in zip(quarters, accs):
+            halve(0, cols, acc)
+        for cols, acc in zip(quarters[:-1], accs):
+            nc.vector.tensor_copy(h[0][:, cols], acc[:])
+        keep_h(0, quarters[-1], accs[-1])
+        for cols in (wide, slice(HALF, S)):
             first_hop(0, cols)
         for t in range(1, PACK):
             acc = h_product(t, whole)
             halve(t, whole, acc)
-            keep_h(t, whole, acc)
+            pieces = [wide, slice(HALF, S)] if t == 1 else [whole]
+            for cols in pieces:
+                nc.scalar.copy(h[t][:, cols], acc[:, cols])
             negate(t - 1)
-            first_hop(t, whole)
+            for cols in pieces:
+                first_hop(t, cols)
             second_hop(t - 1)
         negate(PACK - 1)
         second_hop(PACK - 1)

from contextlib import ExitStack

import concourse.mybir as mybir

K, T, S, N, H, W = 512, 2048, 512, 512, 512, 256
FLOPS = 2 * K * H * S + 2 * H * N * S

F32 = mybir.dt.float32
BF16 = mybir.dt.bfloat16
I32 = mybir.dt.int32
U32 = mybir.dt.uint32
U16 = mybir.dt.uint16
U8 = mybir.dt.uint8
FP8X4 = mybir.dt.float8_e4m3fn_x4
ACT = mybir.ActivationFunctionType
ALU = mybir.AluOpType

P = 128
PACK = 4
HALF = S // 2
COLS16 = HALF // 16
SLOT_ORDER = (0, 2, 3, 1)


def tile_picked_laypolarhop_none_p_kernel(
    tc, x_words, x_scales, w1, gn, w2, offs, n1, n2, n3, n4, out
):
    nc = tc.nc
    with ExitStack() as ctx:
        lists = ctx.enter_context(tc.tile_pool(name="lists", bufs=1))
        keep = ctx.enter_context(tc.tile_pool(name="keep", bufs=1))
        ring = ctx.enter_context(tc.tile_pool(name="ring", bufs=2))
        psum = ctx.enter_context(tc.psum_pool(name="psum", bufs=8))

        def halves():
            return [(a, slice(a * HALF, (a + 1) * HALF), slice(a * COLS16, (a + 1) * COLS16)) for a in range(2)]

        offs_sb = lists.tile([P, S // 16], U16, name="offs_sb")
        n1_sb = lists.tile([P, W // 16], U16, name="n1_sb")
        n2_sb = lists.tile([P, W // 16], U16, name="n2_sb")
        n3_sb = lists.tile([P, S // 16], U16, name="n3_sb")
        n4_sb = lists.tile([P, S // 16], U16, name="n4_sb")
        w1_raw = keep.tile([P, PACK, H], F32, name="w1_raw")
        w2_raw = keep.tile([P, PACK, N], F32, name="w2_raw")
        x_tab = keep.tile([P, T], U32, name="x_tab", tag="x_tab", align_bytes=64)
        xs_tab = keep.tile([P, T], U8, name="xs_tab")
        gain = keep.tile([P, PACK], F32, name="gain")

        nc.vector.memset(xs_tab[:].bitcast(I32), 0)
        nc.sync.dma_start(w1_raw[:], w1.rearrange("(p j) c -> p j c", j=PACK))
        nc.sync.dma_start(offs_sb[:], offs)
        for q in range(4):
            nc.sync.dma_start(
                xs_tab[32 * q : 32 * q + 4, :].bitcast(I32), x_scales[0, 4 * q : 4 * q + 4, :].bitcast(I32)
            )
        nc.sync.dma_start(x_tab[:].bitcast(I32), x_words[0].rearrange("p n t -> p (n t)").bitcast(I32))
        sixteenth = keep.tile([P, 1], F32, name="sixteenth")
        nc.vector.memset(sixteenth[:], 0.0625)
        quarter = keep.tile([P, 1], F32, name="quarter")
        nc.scalar.activation(quarter[:], sixteenth[:], ACT.Sqrt)
        nc.sync.dma_start(n1_sb[:], n1)
        nc.sync.dma_start(n2_sb[:], n2)
        nc.sync.dma_start(w2_raw[:], w2.rearrange("(p j) c -> p j c", j=PACK))
        nc.sync.dma_start(gain[:], gn.rearrange("(p t) o -> p (t o)", t=PACK))
        nc.sync.dma_start(n3_sb[:], n3)
        nc.sync.dma_start(n4_sb[:], n4)

        def deal(engine_copy, grouped, raw, m0, m1):
            engine_copy(
                grouped[:].rearrange("p (t m j) -> p m t j", t=PACK, j=PACK)[:, m0:m1],
                raw[:].rearrange("p j (m t) -> p m t j", t=PACK)[:, m0:m1],
            )

        xg_scales = keep.tile([P, S], U8, name="xg_scales", align_bytes=64)

        w1_bf = keep.tile([P, PACK * H], BF16, name="w1_bf", align_bytes=64)
        w1_to = w1_bf[:].rearrange("p (t m j) -> p m t j", t=PACK, j=PACK)
        w1_from = w1_raw[:].rearrange("p j (m t) -> p m t j", t=PACK)
        nc.vector.tensor_copy(w1_to[:, :, 0], w1_from[:, :, 0])
        nc.scalar.copy(w1_to[:, :, 1:], w1_from[:, :, 1:])
        nc.vector.tensor_copy(xg_scales[:], xs_tab[:].indirect(offs_sb[:]))
        w1_codes = keep.tile([P, P], U32, name="w1_codes", align_bytes=64)
        w1_scales = keep.tile([P, H], U8, name="w1_scales", align_bytes=64)
        nc.vector.quantize_mx(w1_codes[:].bitcast(FP8X4), w1_scales[:, :P], w1_bf[:, : PACK * P])

        xg_words = keep.tile([P, S], U32, name="xg_words", align_bytes=64)
        for a, cols, lcols in halves():
            nc.vector.tensor_copy(xg_words[:, cols], x_tab[:].indirect(offs_sb[:, lcols]))

        w1_rest = keep.tile([P, H - P], U32, name="w1_rest", tag="x_tab", align_bytes=64)
        for c0, c1 in ((P, 2 * P), (2 * P, H)):
            nc.vector.quantize_mx(
                w1_rest[:, c0 - P : c1 - P].bitcast(FP8X4), w1_scales[:, c0:c1], w1_bf[:, PACK * c0 : PACK * c1]
            )
        w1_tiles = [w1_codes[:]] + [w1_rest[:, t * P : (t + 1) * P] for t in range(PACK - 1)]

        def product(codes, scales, t, rhs, rhs_scales, cols, width):
            acc = psum.tile([P, width], F32, name="acc")
            m = slice(t * P, (t + 1) * P)
            nc.tensor.matmul_mx(
                acc[:], lhsT=codes[t].bitcast(FP8X4), lhsT_scale=scales[:, m],
                rhs=rhs[:, cols].bitcast(FP8X4), rhs_scale=rhs_scales[:, cols], start=True, stop=True,
            )
            return acc

        y = keep.tile([P, S], F32, name="y")
        pair = keep.tile([P, 2 * W], F32, name="pair")
        scratch = [keep.tile([P, W], F32, name=f"scratch{b}") for b in range(2)]
        d = {t: keep.tile([P, S], F32, name=f"d{t}", tag=f"d{t}", align_bytes=64) for t in SLOT_ORDER}
        first = SLOT_ORDER[0]
        for cols in (slice(0, HALF), slice(HALF, HALF + P), slice(HALF + P, S)):
            acc = product(w1_tiles, w1_scales, first, xg_words, xg_scales, cols, cols.stop - cols.start)
            nc.scalar.copy(y[:, cols], acc[:])

        def make_y(t):
            acc = product(w1_tiles, w1_scales, t, xg_words, xg_scales, slice(0, S), S)
            nc.scalar.copy(y[:], acc[:])

        z_bf = keep.tile([P, S, PACK], BF16, name="z_bf", align_bytes=64)
        w2_bf = keep.tile([P, PACK * N], BF16, name="w2_bf", align_bytes=64)
        roots = {}

        def put_roots(t):
            nc.vector.tensor_copy(d[t][:].indirect(n1_sb[:]), roots[t][:])

        def write_z(t, cols):
            nc.scalar.activation(z_bf[:, cols, t], d[t][:, cols], ACT.Copy, scale=gain[:, t : t + 1])

        w2_codes = keep.tile([P, 2 * P], U32, name="w2_codes", align_bytes=64)
        w2_scales = keep.tile([P, N], U8, name="w2_scales", align_bytes=64)

        for i, t in enumerate(SLOT_ORDER):
            last = i == PACK - 1
            minus_half, radicand = scratch[(i + 1) % 2], scratch[i % 2]
            nc.vector.tensor_copy(pair[:, :W], y[:].indirect(n1_sb[:]))
            nc.vector.tensor_copy(pair[:, W:], y[:].indirect(n2_sb[:]))
            squares = ring.tile([P, 2 * W], F32, name="squares")
            nc.scalar.activation(squares[:], pair[:], ACT.Square)
            nc.scalar.activation(minus_half[:], pair[:, :W], ACT.Copy, scale=-0.5)
            nc.gpsimd.tensor_tensor(radicand[:], squares[:, :W], squares[:, W:], ALU.add)
            if i > 0:
                put_roots(SLOT_ORDER[i - 1])
            nc.vector.tensor_tensor(d[t][:].indirect(n2_sb[:]), pair[:, W:], minus_half[:], ALU.add)
            if last:
                deal(nc.scalar.copy, w2_bf, w2_raw, 32 * i, 32 * (i + 1))
            else:
                make_y(SLOT_ORDER[i + 1])
            roots[t] = ring.tile([P, W], F32, name="root")
            nc.scalar.activation(roots[t][:], radicand[:], ACT.Sqrt, bias=quarter[:])
            if i > 0:
                write_z(SLOT_ORDER[i - 1], slice(0, S))
            if not last:
                deal(nc.scalar.copy, w2_bf, w2_raw, 32 * i, 32 * (i + 1))

        nc.vector.quantize_mx(w2_codes[:].bitcast(FP8X4), w2_scales[:, : 2 * P], w2_bf[:, : PACK * 2 * P])

        t = SLOT_ORDER[-1]
        put_roots(t)
        early, wide, late = slice(HALF, HALF + P), slice(0, HALF), slice(HALF + P, S)
        quarters = [slice(c * P, (c + 1) * P) for c in (0, 2, 1, 3)]
        for cols in quarters[0::2]:
            nc.vector.tensor_scalar(z_bf[:, cols, t], d[t][:, cols], gain[:, t : t + 1], None, ALU.mult)
        for cols in quarters[1::2]:
            write_z(t, cols)

        z_codes = keep.tile([P, S], U32, name="z_codes", align_bytes=64)
        z_scales = keep.tile([P, S], U8, name="z_scales", align_bytes=64)
        for cols in quarters:
            nc.vector.quantize_mx(
                z_codes[:, cols].bitcast(FP8X4), z_scales[:, cols], z_bf[:, cols, :].rearrange("p s j -> p (s j)")
            )

        w2_rest = keep.tile([P, 2 * P], U32, name="w2_rest", tag=f"d{t}", align_bytes=64)
        nc.vector.quantize_mx(w2_rest[:].bitcast(FP8X4), w2_scales[:, 2 * P :], w2_bf[:, PACK * 2 * P :])
        w2_tiles = [w2_codes[:, :P], w2_codes[:, P:], w2_rest[:, :P], w2_rest[:, P:]]

        whole = slice(0, S)
        half_win = [keep.tile([P, S if t == 0 else 2 * S], F32, name=f"half_win{t}") for t in range(PACK)]
        minus_win = [keep.tile([P, 2 * S if t in (1, 2) else S], F32, name=f"minus_win{t}") for t in range(PACK)]
        h_last = keep.tile([P, S], F32, name="h_last")
        st_late = [keep.tile([P, S], F32, name=f"st_late{t}") for t in range(2)]
        h = [half_win[1][:, S:], half_win[2][:, S:], half_win[3][:, S:], h_last[:]]
        st = [minus_win[1][:, S:], minus_win[2][:, S:], st_late[0][:], st_late[1][:]]
        res = [keep.tile([P, S], F32, name=f"res{t}") for t in range(PACK)]
        out_rows = out.rearrange("(p t) n -> p t n", t=PACK)

        def entries(cols):
            return slice(cols.start // 16, cols.stop // 16)

        def h_product(t, cols):
            return product(w2_tiles, w2_scales, t, z_codes, z_scales, cols, cols.stop - cols.start)

        def halve(t, cols, acc):
            nc.scalar.activation(half_win[t][:, cols], acc[:], ACT.Copy, scale=0.5)

        def keep_h(t, cols, acc):
            nc.scalar.copy(h[t][:, cols], acc[:])

        def first_hop(t, cols):
            nc.vector.tensor_tensor(st[t][:, cols], half_win[t][:].indirect(n3_sb[:, entries(cols)]), h[t][:, cols], ALU.add)

        def negate(t):
            nc.scalar.activation(minus_win[t][:, :S], st[t], ACT.Copy, scale=-1.0)

        def second_hop(t):
            pieces = [whole] if t in (1, 2) else [wide, slice(HALF, S)] if t == 0 else [wide, early, late]
            for cols in pieces:
                nc.vector.tensor_tensor(
                    res[t][:, cols], minus_win[t][:].indirect(n4_sb[:, entries(cols)]), st[t][:, cols], ALU.add
                )
                nc.sync.dma_start(out_rows[:, t, cols], res[t][:, cols])

        accs = [h_product(0, cols) for cols in quarters]
        for cols, acc in zip(quarters, accs):
            halve(0, cols, acc)
        for cols, acc in zip(quarters[:-1], accs):
            nc.vector.tensor_copy(h[0][:, cols], acc[:])
        keep_h(0, quarters[-1], accs[-1])
        for cols in (wide, slice(HALF, S)):
            first_hop(0, cols)
        for t in range(1, PACK):
            acc = h_product(t, whole)
            halve(t, whole, acc)
            pieces = [wide, slice(HALF, S)] if t == 1 else [whole]
            for cols in pieces:
                nc.scalar.copy(h[t][:, cols], acc[:, cols])
            negate(t - 1)
            for cols in pieces:
                first_hop(t, cols)
            second_hop(t - 1)
        negate(PACK - 1)
        second_hop(PACK - 1)
